import numpy as np
import ml_dtypes


def mxq(x, axis, fmt="e4m3"):
    dtype, down = {"e4m3": (ml_dtypes.float8_e4m3fn, 7), "e5m2": (ml_dtypes.float8_e5m2, 14)}[fmt]
    v = np.moveaxis(np.asarray(x, np.float32).astype(ml_dtypes.bfloat16).astype(np.float64), axis, -1)
    blocks = v.reshape(v.shape[:-1] + (-1, 32))
    amax = np.abs(blocks).max(-1, keepdims=True)
    byte = np.maximum(np.where(amax > 0, np.frexp(amax)[1] - 1 + 127, 0) - down, 1)
    scale = np.exp2(byte - 127.0)
    codes = (blocks / scale).astype(np.float32).astype(dtype).astype(np.float64)
    return np.moveaxis((codes * scale).reshape(v.shape), -1, axis)


WIDE = False


def mx_kscale(k):
    if not WIDE:
        return np.ones(k)
    levels = np.array([10, -10, 5, -5, 0])
    if k % 512:
        return np.exp2(np.random.permutation(np.resize(levels, k // 32))).repeat(32)
    a = np.empty((k // 512, 16))
    for p in range(k // 512):
        a[p, :8] = np.random.permutation(np.resize(levels, 8))
        for g in range(8):
            far = levels[np.abs(levels - a[p, g]) >= 10]
            a[p, g + 8] = far[np.random.randint(len(far))]
    return np.exp2(a.ravel()).repeat(32)


def f64(x):
    return np.asarray(x).astype(np.float64)


def striped(idx):
    return np.tile(idx.reshape(-1, 16).T, (8, 1)).astype(np.uint16)


def unstriped(offs):
    return offs[:16].T.reshape(-1).astype(np.int64)


def striped8(idx):
    return np.concatenate([x.reshape(-1, 16).T for x in idx]).astype(np.uint16)


def runs(offs, k):
    lists = np.stack([offs[16 * r : 16 * r + 16].T.reshape(-1) for r in range(8)]).astype(np.int64)
    return lists[np.arange(k) % 512 // 64]


def pack_weight(w):
    k, n = w.shape
    w = f64(np.asarray(w, np.float32).astype(ml_dtypes.bfloat16)).reshape(k // 32, 32, n)
    amax = np.abs(w).max(1)
    byte = np.clip(np.where(amax > 0, np.frexp(amax)[1] - 1 + 127 - 7, 1), 1, 254)
    scaled = (w * np.exp2(127.0 - byte)[:, None, :]).reshape(k, n).astype(np.float32)
    words = np.ascontiguousarray(scaled.reshape(k // 512, 128, 4, n).transpose(0, 1, 3, 2)).astype(ml_dtypes.float8_e4m3fn).view(np.uint8)
    return words, np.ascontiguousarray(byte.astype(np.uint8).reshape(k // 512, 16, n))


def unpack_weight(words, scales):
    g, p, n, _ = words.shape
    vals = np.ascontiguousarray(words).view(ml_dtypes.float8_e4m3fn).astype(np.float64) * np.repeat(np.exp2(scales.astype(np.float64) - 127.0), 8, axis=1)[..., None]
    return vals.transpose(0, 1, 3, 2).reshape(g * 512, n)

def planes(y):
    n, m = y.shape
    v = y.astype(np.float32).astype(ml_dtypes.bfloat16).astype(np.float64).reshape(n // 32, 32, m)
    top = np.abs(v).max(1)
    byte = np.clip(np.where(top > 0, np.frexp(top)[1] - 1 + 127 - 7, 1), 1, 254)
    codes = (v * np.exp2(127.0 - byte)[:, None, :]).reshape(n, m).astype(np.float32).astype(ml_dtypes.float8_e4m3fn).view(np.uint8)
    words = codes.reshape(n // 512, 128, 4, m).transpose(0, 1, 3, 2)
    return np.ascontiguousarray(words), np.ascontiguousarray(byte.astype(np.uint8).reshape(n // 512, 16, m))


K, T, S, N, H = 512, 2048, 512, 512, 512


def setup_inputs():
    n = np.random.standard_normal
    s = mx_kscale(K)[:, None]
    u = mx_kscale(H)
    packed_xT = pack_weight(n((K, T)) * s)
    packed_w1 = pack_weight(n((K, H)) / np.sqrt(K) / s)
    packed_w2 = pack_weight(n((H, N)) / np.sqrt(2 * H) / u[:, None])
    packed_w3 = pack_weight(n((H, N)) / np.sqrt(2 * H) / u[:, None])
    return {
        "x_words": packed_xT[0],
        "x_scales": packed_xT[1],
        "w1_words": packed_w1[0],
        "w1_scales": packed_w1[1],
        "gn": (np.random.uniform(0.5, 1.5, (H, 1)) * u[:, None]).astype(np.float32),
        "gm": (np.random.uniform(0.5, 1.5, (H, 1)) * u[:, None]).astype(np.float32),
        "w2_words": packed_w2[0],
        "w2_scales": packed_w2[1],
        "w3_words": packed_w3[0],
        "w3_scales": packed_w3[1],
        "offs": striped(np.random.permutation(T)[:S]),
        "n1": striped8(np.stack([np.random.permutation(S) for _ in range(8)])),
        "n2": striped8(np.stack([np.random.permutation(S) for _ in range(8)])),
        "n3": striped8(np.stack([np.random.permutation(S) for _ in range(8)])),
        "n4": striped8(np.stack([np.random.permutation(S) for _ in range(8)])),
        "n5": striped8(np.stack([np.random.permutation(S) for _ in range(8)])),
        "n6": striped8(np.stack([np.random.permutation(S) for _ in range(8)])),
        "n7": striped8(np.stack([np.random.permutation(S) for _ in range(8)])),
    }


def reference(x_words, x_scales, w1_words, w1_scales, gn, gm, w2_words, w2_scales, w3_words, w3_scales, offs, n1, n2, n3, n4, n5, n6, n7):
    xq = unpack_weight(x_words, x_scales)[:, unstriped(offs)]
    y = unpack_weight(w1_words, w1_scales).T @ xq
    st = y - (y[np.arange(H)[:, None], runs(n1, H)])
    su = np.maximum(st, st[np.arange(H)[:, None], runs(n2, H)])
    z = f64(gn) * (su + 0.5 * (su[np.arange(H)[:, None], runs(n3, H)]))
    z2 = f64(gm) * ((y * (y[np.arange(H)[:, None], runs(n4, H)])) * (np.tanh(y[np.arange(H)[:, None], runs(n5, H)])))
    h = unpack_weight(w2_words, w2_scales).T @ mxq(z, 0, "e4m3") + unpack_weight(w3_words, w3_scales).T @ mxq(z2, 0, "e4m3")
    out_0 = h - (np.minimum(h[np.arange(N)[:, None], runs(n6, N)], h[np.arange(N)[:, None], runs(n7, N)]))
    return (out_0,) + planes(out_0)

@@ -1,0 +1,312 @@
+from contextlib import ExitStack
+
+import concourse.mybir as mybir
+
+F32 = mybir.dt.float32
+BF16 = mybir.dt.bfloat16
+I32 = mybir.dt.int32
+U32 = mybir.dt.uint32
+U16 = mybir.dt.uint16
+U8 = mybir.dt.uint8
+FP8X4 = mybir.dt.float8_e4m3fn_x4
+ALU = mybir.AluOpType
+ACT = mybir.ActivationFunctionType
+
+P = 128
+PACK = 4
+T = 2048
+S = 512
+HALF = S // 2
+FLOPS = 3 * 2 * 512 * 512 * 512
+
+
+def tile_picked_jointhreecubeunder_none_po_kernel(
+    tc, x_words, x_scales, w1_words, w1_scales, gn, gm, w2_words, w2_scales, w3_words, w3_scales,
+    offs, n1, n2, n3, n4, n5, n6, n7, out_0, out_1, out_2,
+):
+    nc = tc.nc
+    with ExitStack() as ctx:
+        sb = ctx.enter_context(tc.tile_pool(name="sb", bufs=1))
+        psum = ctx.enter_context(tc.psum_pool(name="psum", bufs=8))
+
+        def new(name, shape, dtype):
+            return sb.tile(shape, dtype, name=name, align_bytes=64)
+
+        def words(dram):
+            return dram[0].rearrange("p n t -> p (n t)").bitcast(I32)
+
+        def load_list(name, dram):
+            lst = new(name, [P, S // 16], U16)
+            nc.sync.dma_start(lst[:], dram)
+            return lst
+
+        def load_scale_rows(queue, plane, dram, row):
+            for q in range(4):
+                queue.dma_start(
+                    plane[32 * q + row : 32 * q + row + 4, :].bitcast(I32),
+                    dram[0, 4 * q : 4 * q + 4, :].bitcast(I32),
+                )
+
+        def entries(lst, cols):
+            return lst[:, cols.start // 16 : cols.stop // 16]
+
+        whole = slice(0, S)
+        halves = [slice(0, HALF), slice(HALF, S)]
+        spare = slice(S, 2 * S)
+
+        xs_raw = new("xs_raw", [P, T], U8)
+        w1s_raw = new("w1s_raw", [P, S], U8)
+        w23s_raw = new("w23s_raw", [P, S], U8)
+        nc.vector.memset(xs_raw[:].bitcast(I32), 0)
+        nc.vector.memset(w1s_raw[:].bitcast(I32), 0)
+        offs_t = load_list("offs_t", offs)
+        w1_raw = new("w1_raw", [P, S], I32)
+        nc.sync.dma_start(w1_raw[:], words(w1_words))
+        xw_raw = new("xw_raw", [P, T], U32)
+        nc.sync.dma_start(xw_raw[:].bitcast(I32), words(x_words))
+        load_scale_rows(nc.scalar, xs_raw, x_scales, 0)
+        load_scale_rows(nc.scalar, w1s_raw, w1_scales, 0)
+        l1 = load_list("l1", n1)
+        l4 = load_list("l4", n4)
+        gains = new("gains", [P, 2, 8], F32)
+        nc.sync.dma_start(gains[:, 0, 0:PACK], gm.rearrange("(p t) o -> p (t o)", t=PACK))
+        l5 = load_list("l5", n5)
+        l2 = load_list("l2", n2)
+        nc.sync.dma_start(gains[:, 1, 0:PACK], gn.rearrange("(p t) o -> p (t o)", t=PACK))
+        l3 = load_list("l3", n3)
+        w23_raw = new("w23_raw", [P, 2, S], I32)
+        nc.sync.dma_start(w23_raw[:, 0, :], words(w2_words))
+        nc.sync.dma_start(w23_raw[:, 1, :], words(w3_words))
+        nc.vector.memset(w23s_raw[:].bitcast(I32), 0)
+        load_scale_rows(nc.sync, w23s_raw, w2_scales, 0)
+        load_scale_rows(nc.sync, w23s_raw, w3_scales, 4)
+        l6 = load_list("l6", n6)
+        l7 = load_list("l7", n7)
+
+        zero = new("zero", [P, 1], F32)
+        nc.vector.memset(zero[:], 0.0)
+        sig0 = new("sig0", [P, 1], F32)
+        nc.scalar.activation(sig0[:], zero[:], ACT.Sigmoid)
+
+        y_win = [new("y_win%d" % t, [P, 2 * S], F32) for t in range(PACK)]
+        st_win = [new("st_win%d" % t, [P, 2 * S], F32) for t in range(PACK)]
+        su_win = [new("su_win%d" % t, [P, 2 * S], F32) for t in range(PACK)]
+        h_win = [new("h_win%d" % t, [P, 2 * S], F32) for t in range(PACK)]
+        nc.vector.memset(y_win[0][:, spare], 0.0)
+        yg_last = new("yg_last", [P, S], F32)
+        y_plain = [st_win[t][:, spare] for t in range(PACK)]
+        y_gain = [y_win[t + 1][:, spare] for t in range(PACK - 1)] + [yg_last[:]]
+        st_got = [h_win[t][:, spare] for t in range(PACK)]
+        su_neg = [su_win[t][:, spare] for t in range(PACK)]
+
+        w1_c = new("w1_c", [P, PACK, P], I32)
+        nc.vector.tensor_copy(w1_c[:].rearrange("p t m -> p m t"), w1_raw[:].rearrange("p (m t) -> p m t", t=PACK))
+        w1_s = new("w1_s", [P, PACK, P], U8)
+        nc.vector.tensor_copy(w1_s[:].rearrange("p t m -> p m t"), w1s_raw[:].rearrange("p (m t) -> p m t", t=PACK))
+        x_s = new("x_s", [P, S], U8)
+        nc.vector.tensor_copy(x_s[:], xs_raw[:].indirect(offs_t[:]))
+        x_c = new("x_c", [P, S], U32)
+        for cols in halves:
+            nc.vector.tensor_copy(x_c[:, cols], xw_raw[:].indirect(entries(offs_t, cols)))
+
+        gm2 = new("gm2", [P, PACK], F32)
+        gn_full = new("gn_full", [P, PACK], F32)
+        gn_half = new("gn_half", [P, PACK], F32)
+        nc.gpsimd.tensor_scalar(gm2[:], gains[:, 0, 0:PACK], 2.0, 0.0, ALU.mult, ALU.add)
+        nc.gpsimd.tensor_scalar(gn_full[:], gains[:, 1, 0:PACK], -1.0, 0.0, ALU.mult, ALU.add)
+        nc.gpsimd.tensor_scalar(gn_half[:], gains[:, 1, 0:PACK], -0.5, 0.0, ALU.mult, ALU.add)
+
+        def y_product(t, cols):
+            acc = psum.tile([P, cols.stop - cols.start], F32, name="acc")
+            nc.tensor.matmul_mx(
+                acc[:], lhsT=w1_c[:, t, :].bitcast(FP8X4), lhsT_scale=w1_s[:, t, :],
+                rhs=x_c[:, cols].bitcast(FP8X4), rhs_scale=x_s[:, cols], start=True, stop=True,
+            )
+            return acc
+
+        y_acc = [[(cols, y_product(0, cols)) for cols in halves]]
+        y_acc += [[(whole, y_product(t, whole))] for t in range(1, PACK)]
+
+        def y_out(t):
+            for i, (cols, acc) in enumerate(y_acc[t]):
+                copy = nc.vector.tensor_copy if i == 1 else nc.scalar.copy
+                copy(y_win[t][:, cols], acc[:])
+                copy(y_plain[t][:, cols], acc[:])
+
+        def y_gain_out(t):
+            for cols, acc in y_acc[t]:
+                nc.scalar.activation(y_gain[t][:, cols], acc[:], ACT.Copy, scale=gm2[:, t : t + 1])
+
+        w23_c = new("w23_c", [P, 2, PACK, P], I32)
+        w23_s = new("w23_s", [P, PACK, P], U8)
+
+        sig = new("sig", [P, PACK, S], F32)
+        prod = new("prod", [P, PACK, S], F32)
+        su_full = new("su_full", [P, PACK, S], F32)
+        z = new("z", [P, PACK, S], F32)
+        z2 = new("z2", [P, PACK, S], F32)
+
+        def step_n1(t):
+            nc.vector.tensor_tensor(st_win[t][:, whole], y_win[t][:].indirect(l1[:]), y_plain[t], ALU.subtract)
+
+        def step_n2(t):
+            nc.vector.tensor_copy(st_got[t], st_win[t][:].indirect(l2[:]))
+
+        def step_min(t):
+            nc.vector.tensor_tensor(su_neg[t], st_win[t][:, whole], st_got[t], ALU.min)
+            nc.scalar.activation(su_win[t][:, whole], su_neg[t], ACT.Copy, scale=gn_half[:, t : t + 1])
+            nc.scalar.activation(su_full[:, t, :], su_neg[t], ACT.Copy, scale=gn_full[:, t : t + 1])
+
+        def step_n3(t):
+            nc.vector.tensor_tensor(z[:, t, :], su_win[t][:].indirect(l3[:]), su_full[:, t, :], ALU.add)
+
+        def step_n4(t):
+            nc.vector.tensor_tensor(prod[:, t, :], y_win[t][:].indirect(l4[:]), y_gain[t], ALU.mult)
+
+        def step_n5(t):
+            nc.scalar.activation(sig[:, t, :], y_win[t][:].indirect(l5[:]), ACT.Sigmoid, scale=2.0)
+
+        def step_z2(t, cols):
+            nc.vector.scalar_tensor_tensor(
+                z2[:, t, cols], sig[:, t, cols], sig0[:], prod[:, t, cols], ALU.subtract, ALU.mult
+            )
+
+        def weave(copy, dst, src, cols, planes):
+            copy(
+                dst[:, :, planes].rearrange("p (c i) t -> p c t i", i=4),
+                src[:, planes, cols].rearrange("p t (c i) -> p c t i", i=4),
+            )
+
+        def quantize(codes, scales, src, cols):
+            nc.vector.quantize_mx(codes[:, cols].bitcast(FP8X4), scales[:, cols], src[:].rearrange("p n t -> p (n t)"))
+
+        low, high, every = slice(0, 2), slice(2, 4), slice(0, 4)
+        z_b = new("z_b", [P, S, PACK], BF16)
+        z_c = new("z_c", [P, S], U32)
+        z_s = new("z_s", [P, S], U8)
+        z2_b = [new("z2_b%d" % i, [P, HALF, PACK], BF16) for i in range(2)]
+        z2_c = [new("z2_c%d" % i, [P, HALF], U32) for i in range(2)]
+        z2_s = [new("z2_s%d" % i, [P, HALF], U8) for i in range(2)]
+        first = halves[0]
+
+        y_out(0)
+        y_gain_out(0)
+        y_out(1)
+        step_n1(0)
+        step_n5(0)
+        step_n4(0)
+        step_n2(0)
+        step_n1(1)
+        y_gain_out(1)
+        y_out(2)
+        step_min(0)
+        step_z2(0, whole)
+        step_n2(1)
+        y_gain_out(2)
+        y_out(3)
+        step_n1(2)
+        step_min(1)
+        step_n3(0)
+        nc.vector.tensor_copy(
+            w23_c[:].rearrange("p w t m -> p w m t"), w23_raw[:].rearrange("p w (m t) -> p w m t", t=PACK)
+        )
+        nc.vector.tensor_copy(w23_s[:].rearrange("p t m -> p m t"), w23s_raw[:].rearrange("p (m t) -> p m t", t=PACK))
+        step_n2(2)
+        y_gain_out(3)
+        step_n5(1)
+        step_n1(3)
+        step_min(2)
+        step_n3(1)
+        step_n5(2)
+        step_n2(3)
+        step_n4(1)
+        step_min(3)
+        step_n3(2)
+        step_n5(3)
+        step_z2(1, whole)
+        for i, cols in enumerate(halves):
+            weave(nc.scalar.copy, z2_b[i], z2, cols, low)
+        step_n3(3)
+        weave(nc.scalar.copy, z_b, z, whole, every)
+        step_n4(2)
+        step_n4(3)
+        step_z2(2, whole)
+        quantize(z_c, z_s, z_b, whole)
+        step_z2(3, halves[0])
+        weave(nc.scalar.copy, z2_b[0], z2, halves[0], high)
+        step_z2(3, halves[1])
+        weave(nc.vector.tensor_copy, z2_b[1], z2, halves[1], high)
+        for i in range(2):
+            quantize(z2_c[i], z2_s[i], z2_b[i], first)
+
+        h_plain = new("h_plain", [P, PACK, S], F32)
+
+        def h_product(t, i):
+            cols = halves[i]
+            acc = psum.tile([P, HALF], F32, name="acc")
+            nc.tensor.matmul_mx(
+                acc[:], lhsT=w23_c[:, 0, t, :].bitcast(FP8X4), lhsT_scale=w23_s[:, t, :],
+                rhs=z_c[:, cols].bitcast(FP8X4), rhs_scale=z_s[:, cols], start=True, stop=False,
+            )
+            nc.tensor.matmul_mx(
+                acc[:], lhsT=w23_c[:, 1, t, :].bitcast(FP8X4), lhsT_scale=w23_s[4:, t, :],
+                rhs=z2_c[i][:].bitcast(FP8X4), rhs_scale=z2_s[i][:], start=False, stop=True,
+            )
+            if t == 0 and i == 1:
+                nc.vector.tensor_scalar(h_win[t][:, cols], acc[:], -1.0, None, ALU.mult)
+                nc.vector.tensor_copy(h_plain[:, t, cols], acc[:])
+            else:
+                nc.scalar.activation(h_win[t][:, cols], acc[:], ACT.Copy, scale=-1.0)
+                nc.scalar.copy(h_plain[:, t, cols], acc[:])
+
+        for t in range(PACK):
+            for i in range(2):
+                h_product(t, i)
+
+        d6 = new("d6", [P, PACK, S], F32)
+        d7 = new("d7", [P, PACK, S], F32)
+        res = new("res", [P, PACK, S], F32)
+        res_b = [new("res_b%d" % i, [P, HALF, PACK], BF16) for i in range(2)]
+        res_c = new("res_c", [P, S], U32)
+        res_s = new("res_s", [P, S], U8)
+        out_rows = out_0.rearrange("(p t) n -> p t n", t=PACK)
+        out_words = words(out_1)
+
+        def step_diff(dst, lst, t, cols):
+            nc.vector.tensor_tensor(dst[:, t, cols], h_win[t][:].indirect(entries(lst, cols)), h_plain[:, t, cols], ALU.add)
+
+        def step_max(t, cols):
+            nc.vector.tensor_tensor(res[:, t, cols], d6[:, t, cols], d7[:, t, cols], ALU.max)
+            nc.sync.dma_start(out_rows[:, t, cols], res[:, t, cols])
+
+        def planes_out(i):
+            cols = halves[i]
+            nc.vector.quantize_mx(
+                res_c[:, cols].bitcast(FP8X4), res_s[:, cols], res_b[i][:].rearrange("p n t -> p (n t)")
+            )
+            nc.sync.dma_start(out_words[:, cols], res_c[:, cols].bitcast(I32))
+
+        step_diff(d6, l6, 0, whole)
+        step_diff(d7, l7, 0, whole)
+        step_diff(d6, l6, 1, whole)
+        step_max(0, whole)
+        step_diff(d7, l7, 1, whole)
+        step_diff(d6, l6, 2, whole)
+        step_max(1, whole)
+        for i, cols in enumerate(halves):
+            weave(nc.scalar.copy, res_b[i], res, cols, low)
+        step_diff(d7, l7, 2, whole)
+        step_diff(d6, l6, 3, halves[0])
+        step_max(2, whole)
+        step_diff(d7, l7, 3, halves[0])
+        step_diff(d6, l6, 3, halves[1])
+        step_max(3, halves[0])
+        weave(nc.scalar.copy, res_b[0], res, halves[0], high)
+        step_diff(d7, l7, 3, halves[1])
+        step_max(3, halves[1])
+        planes_out(0)
+        weave(nc.vector.tensor_copy, res_b[1], res, halves[1], high)
+        planes_out(1)
+        for q in range(4):
+            queue = nc.sync if q < 2 else nc.scalar
+            queue.dma_start(out_2[0, 4 * q : 4 * q + 4, :].bitcast(I32), res_s[32 * q : 32 * q + 4, :].bitcast(I32))

@@ -47,26 +47,33 @@ def tile_picked_jointhreecubeunder_none_po_kernel(
                     dram[0, 4 * q : 4 * q + 4, :].bitcast(I32),
                 )
 
+        def deal(dst, src):
+            nc.vector.tensor_copy(dst[:].rearrange("p t m -> p m t"), src[:].rearrange("p (m t) -> p m t", t=PACK))
+
         def entries(lst, cols):
             return lst[:, cols.start // 16 : cols.stop // 16]
 
         whole = slice(0, S)
         halves = [slice(0, HALF), slice(HALF, S)]
+        quarters = [slice(HALF, HALF + P), slice(HALF + P, S)]
         spare = slice(S, 2 * S)
 
         xs_raw = new("xs_raw", [P, T], U8)
         w1s_raw = new("w1s_raw", [P, S], U8)
         w23s_raw = new("w23s_raw", [P, S], U8)
-        nc.vector.memset(xs_raw[:].bitcast(I32), 0)
-        nc.vector.memset(w1s_raw[:].bitcast(I32), 0)
+        nc.vector.memset(xs_raw[:].bitcast(I32)[:, 0:320], 0)
+        nc.gpsimd.memset(xs_raw[:].bitcast(I32)[:, 320:512], 0)
+        nc.gpsimd.memset(w1s_raw[:].bitcast(I32), 0)
         offs_t = load_list("offs_t", offs)
         w1_raw = new("w1_raw", [P, S], I32)
         nc.sync.dma_start(w1_raw[:], words(w1_words))
+        load_scale_rows(nc.sync, xs_raw, x_scales, 0)
         xw_raw = new("xw_raw", [P, T], U32)
         nc.sync.dma_start(xw_raw[:].bitcast(I32), words(x_words))
-        load_scale_rows(nc.scalar, xs_raw, x_scales, 0)
-        load_scale_rows(nc.scalar, w1s_raw, w1_scales, 0)
+        load_scale_rows(nc.sync, w1s_raw, w1_scales, 0)
         l1 = load_list("l1", n1)
+        w2_raw = new("w2_raw", [P, S], I32)
+        nc.sync.dma_start(w2_raw[:], words(w2_words))
         l4 = load_list("l4", n4)
         gains = new("gains", [P, 2, 8], F32)
         nc.sync.dma_start(gains[:, 0, 0:PACK], gm.rearrange("(p t) o -> p (t o)", t=PACK))
@@ -74,9 +81,8 @@ def tile_picked_jointhreecubeunder_none_po_kernel(
         l2 = load_list("l2", n2)
         nc.sync.dma_start(gains[:, 1, 0:PACK], gn.rearrange("(p t) o -> p (t o)", t=PACK))
         l3 = load_list("l3", n3)
-        w23_raw = new("w23_raw", [P, 2, S], I32)
-        nc.sync.dma_start(w23_raw[:, 0, :], words(w2_words))
-        nc.sync.dma_start(w23_raw[:, 1, :], words(w3_words))
+        w3_raw = new("w3_raw", [P, S], I32)
+        nc.sync.dma_start(w3_raw[:], words(w3_words))
         nc.vector.memset(w23s_raw[:].bitcast(I32), 0)
         load_scale_rows(nc.sync, w23s_raw, w2_scales, 0)
         load_scale_rows(nc.sync, w23s_raw, w3_scales, 4)
@@ -100,14 +106,17 @@ def tile_picked_jointhreecubeunder_none_po_kernel(
         su_neg = [su_win[t][:, spare] for t in range(PACK)]
 
         w1_c = new("w1_c", [P, PACK, P], I32)
-        nc.vector.tensor_copy(w1_c[:].rearrange("p t m -> p m t"), w1_raw[:].rearrange("p (m t) -> p m t", t=PACK))
+        deal(w1_c, w1_raw)
         w1_s = new("w1_s", [P, PACK, P], U8)
-        nc.vector.tensor_copy(w1_s[:].rearrange("p t m -> p m t"), w1s_raw[:].rearrange("p (m t) -> p m t", t=PACK))
+        deal(w1_s, w1s_raw)
         x_s = new("x_s", [P, S], U8)
         nc.vector.tensor_copy(x_s[:], xs_raw[:].indirect(offs_t[:]))
         x_c = new("x_c", [P, S], U32)
         for cols in halves:
             nc.vector.tensor_copy(x_c[:, cols], xw_raw[:].indirect(entries(offs_t, cols)))
+
+        w2_c = new("w2_c", [P, PACK, P], I32)
+        deal(w2_c, w2_raw)
 
         gm2 = new("gm2", [P, PACK], F32)
         gn_full = new("gn_full", [P, PACK], F32)
@@ -124,12 +133,12 @@ def tile_picked_jointhreecubeunder_none_po_kernel(
             )
             return acc
 
-        y_acc = [[(cols, y_product(0, cols)) for cols in halves]]
+        y_acc = [[(cols, y_product(0, cols)) for cols in halves[:1] + quarters]]
         y_acc += [[(whole, y_product(t, whole))] for t in range(1, PACK)]
 
         def y_out(t):
             for i, (cols, acc) in enumerate(y_acc[t]):
-                copy = nc.vector.tensor_copy if i == 1 else nc.scalar.copy
+                copy = nc.vector.tensor_copy if i == 2 else nc.scalar.copy
                 copy(y_win[t][:, cols], acc[:])
                 copy(y_plain[t][:, cols], acc[:])
 
@@ -137,7 +146,7 @@ def tile_picked_jointhreecubeunder_none_po_kernel(
             for cols, acc in y_acc[t]:
                 nc.scalar.activation(y_gain[t][:, cols], acc[:], ACT.Copy, scale=gm2[:, t : t + 1])
 
-        w23_c = new("w23_c", [P, 2, PACK, P], I32)
+        w3_c = new("w3_c", [P, PACK, P], I32)
         w23_s = new("w23_s", [P, PACK, P], U8)
 
         sig = new("sig", [P, PACK, S], F32)
@@ -160,8 +169,8 @@ def tile_picked_jointhreecubeunder_none_po_kernel(
         def step_n3(t):
             nc.vector.tensor_tensor(z[:, t, :], su_win[t][:].indirect(l3[:]), su_full[:, t, :], ALU.add)
 
-        def step_n4(t):
-            nc.vector.tensor_tensor(prod[:, t, :], y_win[t][:].indirect(l4[:]), y_gain[t], ALU.mult)
+        def step_n4(t, cols):
+            nc.vector.tensor_tensor(prod[:, t, cols], y_win[t][:].indirect(entries(l4, cols)), y_gain[t][:, cols], ALU.mult)
 
         def step_n5(t):
             nc.scalar.activation(sig[:, t, :], y_win[t][:].indirect(l5[:]), ACT.Sigmoid, scale=2.0)
@@ -194,7 +203,7 @@ def tile_picked_jointhreecubeunder_none_po_kernel(
         y_out(1)
         step_n1(0)
         step_n5(0)
-        step_n4(0)
+        step_n4(0, whole)
         step_n2(0)
         step_n1(1)
         y_gain_out(1)
@@ -207,10 +216,8 @@ def tile_picked_jointhreecubeunder_none_po_kernel(
         step_n1(2)
         step_min(1)
         step_n3(0)
-        nc.vector.tensor_copy(
-            w23_c[:].rearrange("p w t m -> p w m t"), w23_raw[:].rearrange("p w (m t) -> p w m t", t=PACK)
-        )
-        nc.vector.tensor_copy(w23_s[:].rearrange("p t m -> p m t"), w23s_raw[:].rearrange("p (m t) -> p m t", t=PACK))
+        deal(w3_c, w3_raw)
+        deal(w23_s, w23s_raw)
         step_n2(2)
         y_gain_out(3)
         step_n5(1)
@@ -219,7 +226,7 @@ def tile_picked_jointhreecubeunder_none_po_kernel(
         step_n3(1)
         step_n5(2)
         step_n2(3)
-        step_n4(1)
+        step_n4(1, whole)
         step_min(3)
         step_n3(2)
         step_n5(3)
@@ -228,40 +235,45 @@ def tile_picked_jointhreecubeunder_none_po_kernel(
             weave(nc.scalar.copy, z2_b[i], z2, cols, low)
         step_n3(3)
         weave(nc.scalar.copy, z_b, z, whole, every)
-        step_n4(2)
-        step_n4(3)
+        step_n4(2, whole)
+        step_n4(3, halves[0])
         step_z2(2, whole)
-        quantize(z_c, z_s, z_b, whole)
         step_z2(3, halves[0])
         weave(nc.scalar.copy, z2_b[0], z2, halves[0], high)
+        step_n4(3, halves[1])
+        quantize(z_c, z_s, z_b, whole)
         step_z2(3, halves[1])
+        quantize(z2_c[0], z2_s[0], z2_b[0], first)
         weave(nc.vector.tensor_copy, z2_b[1], z2, halves[1], high)
-        for i in range(2):
-            quantize(z2_c[i], z2_s[i], z2_b[i], first)
+        quantize(z2_c[1], z2_s[1], z2_b[1], first)
 
         h_plain = new("h_plain", [P, PACK, S], F32)
 
-        def h_product(t, i):
-            cols = halves[i]
-            acc = psum.tile([P, HALF], F32, name="acc")
+        def h_product(t, cols, on_vector=False):
+            i = cols.start // HALF
+            local = slice(cols.start - i * HALF, cols.stop - i * HALF)
+            acc = psum.tile([P, cols.stop - cols.start], F32, name="acc")
             nc.tensor.matmul_mx(
-                acc[:], lhsT=w23_c[:, 0, t, :].bitcast(FP8X4), lhsT_scale=w23_s[:, t, :],
+                acc[:], lhsT=w2_c[:, t, :].bitcast(FP8X4), lhsT_scale=w23_s[:, t, :],
                 rhs=z_c[:, cols].bitcast(FP8X4), rhs_scale=z_s[:, cols], start=True, stop=False,
             )
             nc.tensor.matmul_mx(
-                acc[:], lhsT=w23_c[:, 1, t, :].bitcast(FP8X4), lhsT_scale=w23_s[4:, t, :],
-                rhs=z2_c[i][:].bitcast(FP8X4), rhs_scale=z2_s[i][:], start=False, stop=True,
+                acc[:], lhsT=w3_c[:, t, :].bitcast(FP8X4), lhsT_scale=w23_s[4:, t, :],
+                rhs=z2_c[i][:, local].bitcast(FP8X4), rhs_scale=z2_s[i][:, local], start=False, stop=True,
             )
-            if t == 0 and i == 1:
+            if on_vector:
                 nc.vector.tensor_scalar(h_win[t][:, cols], acc[:], -1.0, None, ALU.mult)
                 nc.vector.tensor_copy(h_plain[:, t, cols], acc[:])
             else:
                 nc.scalar.activation(h_win[t][:, cols], acc[:], ACT.Copy, scale=-1.0)
                 nc.scalar.copy(h_plain[:, t, cols], acc[:])
 
-        for t in range(PACK):
-            for i in range(2):
-                h_product(t, i)
+        h_product(0, halves[0])
+        h_product(0, quarters[0])
+        h_product(0, quarters[1], on_vector=True)
+        for t in range(1, PACK):
+            for cols in halves:
+                h_product(t, cols)
 
         d6 = new("d6", [P, PACK, S], F32)
         d7 = new("d7", [P, PACK, S], F32)

@@ -100,7 +100,8 @@ def tile_picked_jointhreecubeunder_none_po_kernel(
         h_win = [new("h_win%d" % t, [P, 2 * S], F32) for t in range(PACK)]
         nc.vector.memset(y_win[0][:, spare], 0.0)
         yg_last = new("yg_last", [P, S], F32)
-        y_plain = [st_win[t][:, spare] for t in range(PACK)]
+        yp_first = new("yp_first", [P, S], F32)
+        y_plain = [yp_first[:]] + [st_win[t][:, spare] for t in range(PACK - 1)]
         y_gain = [y_win[t + 1][:, spare] for t in range(PACK - 1)] + [yg_last[:]]
         st_got = [h_win[t][:, spare] for t in range(PACK)]
         su_neg = [su_win[t][:, spare] for t in range(PACK)]
@@ -149,7 +150,8 @@ def tile_picked_jointhreecubeunder_none_po_kernel(
         w3_c = new("w3_c", [P, PACK, P], I32)
         w23_s = new("w23_s", [P, PACK, P], U8)
 
-        sig = new("sig", [P, PACK, S], F32)
+        sig_own = new("sig_own", [P, PACK - 1, S], F32)
+        sig = [sig_own[:, 0, :], sig_own[:, 1, :], st_win[PACK - 1][:, spare], sig_own[:, 2, :]]
         prod = new("prod", [P, PACK, S], F32)
         su_full = new("su_full", [P, PACK, S], F32)
         z = new("z", [P, PACK, S], F32)
@@ -163,21 +165,23 @@ def tile_picked_jointhreecubeunder_none_po_kernel(
 
         def step_min(t):
             nc.vector.tensor_tensor(su_neg[t], st_win[t][:, whole], st_got[t], ALU.min)
+
+        def step_gain(t):
             nc.scalar.activation(su_win[t][:, whole], su_neg[t], ACT.Copy, scale=gn_half[:, t : t + 1])
             nc.scalar.activation(su_full[:, t, :], su_neg[t], ACT.Copy, scale=gn_full[:, t : t + 1])
 
-        def step_n3(t):
-            nc.vector.tensor_tensor(z[:, t, :], su_win[t][:].indirect(l3[:]), su_full[:, t, :], ALU.add)
+        def step_n3(t, cols):
+            nc.vector.tensor_tensor(z[:, t, cols], su_win[t][:].indirect(entries(l3, cols)), su_full[:, t, cols], ALU.add)
 
         def step_n4(t, cols):
             nc.vector.tensor_tensor(prod[:, t, cols], y_win[t][:].indirect(entries(l4, cols)), y_gain[t][:, cols], ALU.mult)
 
         def step_n5(t):
-            nc.scalar.activation(sig[:, t, :], y_win[t][:].indirect(l5[:]), ACT.Sigmoid, scale=2.0)
+            nc.scalar.activation(sig[t], y_win[t][:].indirect(l5[:]), ACT.Sigmoid, scale=2.0)
 
         def step_z2(t, cols):
             nc.vector.scalar_tensor_tensor(
-                z2[:, t, cols], sig[:, t, cols], sig0[:], prod[:, t, cols], ALU.subtract, ALU.mult
+                z2[:, t, cols], sig[t][:, cols], sig0[:], prod[:, t, cols], ALU.subtract, ALU.mult
             )
 
         def weave(copy, dst, src, cols, planes):
@@ -190,62 +194,54 @@ def tile_picked_jointhreecubeunder_none_po_kernel(
             nc.vector.quantize_mx(codes[:, cols].bitcast(FP8X4), scales[:, cols], src[:].rearrange("p n t -> p (n t)"))
 
         low, high, every = slice(0, 2), slice(2, 4), slice(0, 4)
-        z_b = new("z_b", [P, S, PACK], BF16)
-        z_c = new("z_c", [P, S], U32)
-        z_s = new("z_s", [P, S], U8)
-        z2_b = [new("z2_b%d" % i, [P, HALF, PACK], BF16) for i in range(2)]
-        z2_c = [new("z2_c%d" % i, [P, HALF], U32) for i in range(2)]
-        z2_s = [new("z2_s%d" % i, [P, HALF], U8) for i in range(2)]
+        z2_b = new("z2_b", [P, S, PACK], BF16)
+        z2_c = new("z2_c", [P, S], U32)
+        z2_s = new("z2_s", [P, S], U8)
+        z_b = [new("z_b%d" % i, [P, HALF, PACK], BF16) for i in range(2)]
+        z_c = [new("z_c%d" % i, [P, HALF], U32) for i in range(2)]
+        z_s = [new("z_s%d" % i, [P, HALF], U8) for i in range(2)]
         first = halves[0]
+        last = PACK - 1
 
         y_out(0)
-        y_gain_out(0)
-        y_out(1)
         step_n1(0)
-        step_n5(0)
-        step_n4(0, whole)
-        step_n2(0)
-        step_n1(1)
-        y_gain_out(1)
-        y_out(2)
-        step_min(0)
-        step_z2(0, whole)
-        step_n2(1)
-        y_gain_out(2)
-        y_out(3)
-        step_n1(2)
-        step_min(1)
-        step_n3(0)
+        for t in range(last):
+            y_gain_out(t)
+            step_n4(t, whole)
+            if t > 0:
+                step_n5(t - 1)
+                step_z2(t - 1, whole)
+            y_out(t + 1)
+            step_n2(t)
+            step_n1(t + 1)
+            step_min(t)
+            if t > 0:
+                step_gain(t - 1)
+                step_n3(t - 1, whole)
         deal(w3_c, w3_raw)
         deal(w23_s, w23s_raw)
-        step_n2(2)
-        y_gain_out(3)
-        step_n5(1)
-        step_n1(3)
-        step_min(2)
-        step_n3(1)
-        step_n5(2)
-        step_n2(3)
-        step_n4(1, whole)
-        step_min(3)
-        step_n3(2)
-        step_n5(3)
-        step_z2(1, whole)
+        y_gain_out(last)
+        step_n4(last, whole)
+        step_n5(last - 1)
+        step_n2(last)
+        step_z2(last - 1, whole)
+        step_min(last)
+        step_n5(last)
+        step_z2(last, whole)
+        step_gain(last - 1)
+        step_n3(last - 1, whole)
+        weave(nc.scalar.copy, z2_b, z2, whole, low)
         for i, cols in enumerate(halves):
-            weave(nc.scalar.copy, z2_b[i], z2, cols, low)
-        step_n3(3)
-        weave(nc.scalar.copy, z_b, z, whole, every)
-        step_n4(2, whole)
-        step_n4(3, halves[0])
-        step_z2(2, whole)
-        step_z2(3, halves[0])
-        weave(nc.scalar.copy, z2_b[0], z2, halves[0], high)
-        step_n4(3, halves[1])
-        quantize(z_c, z_s, z_b, whole)
-        step_z2(3, halves[1])
-        quantize(z2_c[0], z2_s[0], z2_b[0], first)
-        weave(nc.vector.tensor_copy, z2_b[1], z2, halves[1], high)
-        quantize(z2_c[1], z2_s[1], z2_b[1], first)
+            weave(nc.scalar.copy, z_b[i], z, cols, low)
+        step_gain(last)
+        weave(nc.scalar.copy, z2_b, z2, whole, high)
+        step_n3(last, halves[0])
+        weave(nc.scalar.copy, z_b[0], z, halves[0], high)
+        step_n3(last, halves[1])
+        quantize(z2_c, z2_s, z2_b, whole)
+        weave(nc.vector.tensor_copy, z_b[1], z, halves[1], high)
+        quantize(z_c[0], z_s[0], z_b[0], first)
+        quantize(z_c[1], z_s[1], z_b[1], first)
 
         h_plain = new("h_plain", [P, PACK, S], F32)
 
@@ -254,12 +250,12 @@ def tile_picked_jointhreecubeunder_none_po_kernel(
             local = slice(cols.start - i * HALF, cols.stop - i * HALF)
             acc = psum.tile([P, cols.stop - cols.start], F32, name="acc")
             nc.tensor.matmul_mx(
-                acc[:], lhsT=w2_c[:, t, :].bitcast(FP8X4), lhsT_scale=w23_s[:, t, :],
-                rhs=z_c[:, cols].bitcast(FP8X4), rhs_scale=z_s[:, cols], start=True, stop=False,
+                acc[:], lhsT=w3_c[:, t, :].bitcast(FP8X4), lhsT_scale=w23_s[4:, t, :],
+                rhs=z2_c[:, cols].bitcast(FP8X4), rhs_scale=z2_s[:, cols], start=True, stop=False,
             )
             nc.tensor.matmul_mx(
-                acc[:], lhsT=w3_c[:, t, :].bitcast(FP8X4), lhsT_scale=w23_s[4:, t, :],
-                rhs=z2_c[i][:, local].bitcast(FP8X4), rhs_scale=z2_s[i][:, local], start=False, stop=True,
+                acc[:], lhsT=w2_c[:, t, :].bitcast(FP8X4), lhsT_scale=w23_s[:, t, :],
+                rhs=z_c[i][:, local].bitcast(FP8X4), rhs_scale=z_s[i][:, local], start=False, stop=True,
             )
             if on_vector:
                 nc.vector.tensor_scalar(h_win[t][:, cols], acc[:], -1.0, None, ALU.mult)

from contextlib import ExitStack

import concourse.mybir as mybir

F32 = mybir.dt.float32
BF16 = mybir.dt.bfloat16
I32 = mybir.dt.int32
U32 = mybir.dt.uint32
U16 = mybir.dt.uint16
U8 = mybir.dt.uint8
FP8X4 = mybir.dt.float8_e4m3fn_x4
ALU = mybir.AluOpType
ACT = mybir.ActivationFunctionType

P = 128
PACK = 4
T = 2048
S = 512
HALF = S // 2
FLOPS = 3 * 2 * 512 * 512 * 512


def tile_picked_jointhreecubeunder_none_po_kernel(
    tc, x_words, x_scales, w1_words, w1_scales, gn, gm, w2_words, w2_scales, w3_words, w3_scales,
    offs, n1, n2, n3, n4, n5, n6, n7, out_0, out_1, out_2,
):
    nc = tc.nc
    with ExitStack() as ctx:
        sb = ctx.enter_context(tc.tile_pool(name="sb", bufs=1))
        psum = ctx.enter_context(tc.psum_pool(name="psum", bufs=8))

        def new(name, shape, dtype):
            return sb.tile(shape, dtype, name=name, align_bytes=64)

        def words(dram):
            return dram[0].rearrange("p n t -> p (n t)").bitcast(I32)

        def load_list(name, dram):
            lst = new(name, [P, S // 16], U16)
            nc.sync.dma_start(lst[:], dram)
            return lst

        def load_scale_rows(queue, plane, dram, row):
            for q in range(4):
                queue.dma_start(
                    plane[32 * q + row : 32 * q + row + 4, :].bitcast(I32),
                    dram[0, 4 * q : 4 * q + 4, :].bitcast(I32),
                )

        def deal(dst, src):
            nc.vector.tensor_copy(dst[:].rearrange("p t m -> p m t"), src[:].rearrange("p (m t) -> p m t", t=PACK))

        def entries(lst, cols):
            return lst[:, cols.start // 16 : cols.stop // 16]

        whole = slice(0, S)
        halves = [slice(0, HALF), slice(HALF, S)]
        quarters = [slice(HALF, HALF + P), slice(HALF + P, S)]
        spare = slice(S, 2 * S)

        xs_raw = new("xs_raw", [P, T], U8)
        w1s_raw = new("w1s_raw", [P, S], U8)
        w23s_raw = new("w23s_raw", [P, S], U8)
        nc.vector.memset(xs_raw[:].bitcast(I32)[:, 0:320], 0)
        nc.gpsimd.memset(xs_raw[:].bitcast(I32)[:, 320:512], 0)
        nc.gpsimd.memset(w1s_raw[:].bitcast(I32), 0)
        offs_t = load_list("offs_t", offs)
        w1_raw = new("w1_raw", [P, S], I32)
        nc.sync.dma_start(w1_raw[:], words(w1_words))
        load_scale_rows(nc.sync, xs_raw, x_scales, 0)
        xw_raw = new("xw_raw", [P, T], U32)
        nc.sync.dma_start(xw_raw[:].bitcast(I32), words(x_words))
        load_scale_rows(nc.sync, w1s_raw, w1_scales, 0)
        l1 = load_list("l1", n1)
        w2_raw = new("w2_raw", [P, S], I32)
        nc.sync.dma_start(w2_raw[:], words(w2_words))
        l4 = load_list("l4", n4)
        gains = new("gains", [P, 2, 8], F32)
        nc.sync.dma_start(gains[:, 0, 0:PACK], gm.rearrange("(p t) o -> p (t o)", t=PACK))
        l5 = load_list("l5", n5)
        l2 = load_list("l2", n2)
        nc.sync.dma_start(gains[:, 1, 0:PACK], gn.rearrange("(p t) o -> p (t o)", t=PACK))
        l3 = load_list("l3", n3)
        w3_raw = new("w3_raw", [P, S], I32)
        nc.sync.dma_start(w3_raw[:], words(w3_words))
        nc.vector.memset(w23s_raw[:].bitcast(I32), 0)
        load_scale_rows(nc.sync, w23s_raw, w2_scales, 0)
        load_scale_rows(nc.sync, w23s_raw, w3_scales, 4)
        l6 = load_list("l6", n6)
        l7 = load_list("l7", n7)

        zero = new("zero", [P, 1], F32)
        nc.vector.memset(zero[:], 0.0)
        sig0 = new("sig0", [P, 1], F32)
        nc.scalar.activation(sig0[:], zero[:], ACT.Sigmoid)

        y_win = [new("y_win%d" % t, [P, 2 * S], F32) for t in range(PACK)]
        st_win = [new("st_win%d" % t, [P, 2 * S], F32) for t in range(PACK)]
        su_win = [new("su_win%d" % t, [P, 2 * S], F32) for t in range(PACK)]
        h_win = [new("h_win%d" % t, [P, 2 * S], F32) for t in range(PACK)]
        nc.vector.memset(y_win[0][:, spare], 0.0)
        yg_last = new("yg_last", [P, S], F32)
        yp_first = new("yp_first", [P, S], F32)
        y_plain = [yp_first[:]] + [st_win[t][:, spare] for t in range(PACK - 1)]
        y_gain = [y_win[t + 1][:, spare] for t in range(PACK - 1)] + [yg_last[:]]
        st_got = [h_win[t][:, spare] for t in range(PACK)]
        su_neg = [su_win[t][:, spare] for t in range(PACK)]

        w1_c = new("w1_c", [P, PACK, P], I32)
        deal(w1_c, w1_raw)
        w1_s = new("w1_s", [P, PACK, P], U8)
        deal(w1_s, w1s_raw)
        x_s = new("x_s", [P, S], U8)
        nc.vector.tensor_copy(x_s[:], xs_raw[:].indirect(offs_t[:]))
        x_c = new("x_c", [P, S], U32)
        for cols in halves:
            nc.vector.tensor_copy(x_c[:, cols], xw_raw[:].indirect(entries(offs_t, cols)))

        w2_c = new("w2_c", [P, PACK, P], I32)
        deal(w2_c, w2_raw)

        gm2 = new("gm2", [P, PACK], F32)
        gn_full = new("gn_full", [P, PACK], F32)
        gn_half = new("gn_half", [P, PACK], F32)
        nc.gpsimd.tensor_scalar(gm2[:], gains[:, 0, 0:PACK], 2.0, 0.0, ALU.mult, ALU.add)
        nc.gpsimd.tensor_scalar(gn_full[:], gains[:, 1, 0:PACK], -1.0, 0.0, ALU.mult, ALU.add)
        nc.gpsimd.tensor_scalar(gn_half[:], gains[:, 1, 0:PACK], -0.5, 0.0, ALU.mult, ALU.add)

        def y_product(t, cols):
            acc = psum.tile([P, cols.stop - cols.start], F32, name="acc")
            nc.tensor.matmul_mx(
                acc[:], lhsT=w1_c[:, t, :].bitcast(FP8X4), lhsT_scale=w1_s[:, t, :],
                rhs=x_c[:, cols].bitcast(FP8X4), rhs_scale=x_s[:, cols], start=True, stop=True,
            )
            return acc

        y_acc = [[(cols, y_product(0, cols)) for cols in halves[:1] + quarters]]
        y_acc += [[(whole, y_product(t, whole))] for t in range(1, PACK)]

        def y_out(t):
            for i, (cols, acc) in enumerate(y_acc[t]):
                copy = nc.vector.tensor_copy if i == 2 else nc.scalar.copy
                copy(y_win[t][:, cols], acc[:])
                copy(y_plain[t][:, cols], acc[:])

        def y_gain_out(t):
            for cols, acc in y_acc[t]:
                nc.scalar.activation(y_gain[t][:, cols], acc[:], ACT.Copy, scale=gm2[:, t : t + 1])

        w3_c = new("w3_c", [P, PACK, P], I32)
        w23_s = new("w23_s", [P, PACK, P], U8)

        sig_own = new("sig_own", [P, PACK - 1, S], F32)
        sig = [sig_own[:, 0, :], sig_own[:, 1, :], st_win[PACK - 1][:, spare], sig_own[:, 2, :]]
        prod = new("prod", [P, PACK, S], F32)
        su_full = new("su_full", [P, PACK, S], F32)
        z = new("z", [P, PACK, S], F32)
        z2 = new("z2", [P, PACK, S], F32)

        def step_n1(t):
            nc.vector.tensor_tensor(st_win[t][:, whole], y_win[t][:].indirect(l1[:]), y_plain[t], ALU.subtract)

        def step_n2(t):
            nc.vector.tensor_copy(st_got[t], st_win[t][:].indirect(l2[:]))

        def step_min(t):
            nc.vector.tensor_tensor(su_neg[t], st_win[t][:, whole], st_got[t], ALU.min)

        def step_gain(t):
            nc.scalar.activation(su_win[t][:, whole], su_neg[t], ACT.Copy, scale=gn_half[:, t : t + 1])
            nc.scalar.activation(su_full[:, t, :], su_neg[t], ACT.Copy, scale=gn_full[:, t : t + 1])

        def step_n3(t, cols):
            nc.vector.tensor_tensor(z[:, t, cols], su_win[t][:].indirect(entries(l3, cols)), su_full[:, t, cols], ALU.add)

        def step_n4(t, cols):
            nc.vector.tensor_tensor(prod[:, t, cols], y_win[t][:].indirect(entries(l4, cols)), y_gain[t][:, cols], ALU.mult)

        def step_n5(t):
            nc.scalar.activation(sig[t], y_win[t][:].indirect(l5[:]), ACT.Sigmoid, scale=2.0)

        def step_z2(t, cols):
            nc.vector.scalar_tensor_tensor(
                z2[:, t, cols], sig[t][:, cols], sig0[:], prod[:, t, cols], ALU.subtract, ALU.mult
            )

        def weave(copy, dst, src, cols, planes):
            copy(
                dst[:, :, planes].rearrange("p (c i) t -> p c t i", i=4),
                src[:, planes, cols].rearrange("p t (c i) -> p c t i", i=4),
            )

        def quantize(codes, scales, src, cols):
            nc.vector.quantize_mx(codes[:, cols].bitcast(FP8X4), scales[:, cols], src[:].rearrange("p n t -> p (n t)"))

        low, high, every = slice(0, 2), slice(2, 4), slice(0, 4)
        z2_b = new("z2_b", [P, S, PACK], BF16)
        z2_c = new("z2_c", [P, S], U32)
        z2_s = new("z2_s", [P, S], U8)
        z_b = [new("z_b%d" % i, [P, HALF, PACK], BF16) for i in range(2)]
        z_c = [new("z_c%d" % i, [P, HALF], U32) for i in range(2)]
        z_s = [new("z_s%d" % i, [P, HALF], U8) for i in range(2)]
        first = halves[0]
        last = PACK - 1

        y_out(0)
        step_n1(0)
        for t in range(last):
            y_gain_out(t)
            step_n4(t, whole)
            if t > 0:
                step_n5(t - 1)
                step_z2(t - 1, whole)
            y_out(t + 1)
            step_n2(t)
            step_n1(t + 1)
            step_min(t)
            if t > 0:
                step_gain(t - 1)
                step_n3(t - 1, whole)
        deal(w3_c, w3_raw)
        deal(w23_s, w23s_raw)
        y_gain_out(last)
        step_n4(last, whole)
        step_n5(last - 1)
        step_n2(last)
        step_z2(last - 1, whole)
        step_min(last)
        step_n5(last)
        step_z2(last, whole)
        step_gain(last - 1)
        step_n3(last - 1, whole)
        weave(nc.scalar.copy, z2_b, z2, whole, low)
        for i, cols in enumerate(halves):
            weave(nc.scalar.copy, z_b[i], z, cols, low)
        step_gain(last)
        weave(nc.scalar.copy, z2_b, z2, whole, high)
        step_n3(last, halves[0])
        weave(nc.scalar.copy, z_b[0], z, halves[0], high)
        step_n3(last, halves[1])
        quantize(z2_c, z2_s, z2_b, whole)
        weave(nc.vector.tensor_copy, z_b[1], z, halves[1], high)
        quantize(z_c[0], z_s[0], z_b[0], first)
        quantize(z_c[1], z_s[1], z_b[1], first)

        h_plain = new("h_plain", [P, PACK, S], F32)

        def h_product(t, cols, on_vector=False):
            i = cols.start // HALF
            local = slice(cols.start - i * HALF, cols.stop - i * HALF)
            acc = psum.tile([P, cols.stop - cols.start], F32, name="acc")
            nc.tensor.matmul_mx(
                acc[:], lhsT=w3_c[:, t, :].bitcast(FP8X4), lhsT_scale=w23_s[4:, t, :],
                rhs=z2_c[:, cols].bitcast(FP8X4), rhs_scale=z2_s[:, cols], start=True, stop=False,
            )
            nc.tensor.matmul_mx(
                acc[:], lhsT=w2_c[:, t, :].bitcast(FP8X4), lhsT_scale=w23_s[:, t, :],
                rhs=z_c[i][:, local].bitcast(FP8X4), rhs_scale=z_s[i][:, local], start=False, stop=True,
            )
            if on_vector:
                nc.vector.tensor_scalar(h_win[t][:, cols], acc[:], -1.0, None, ALU.mult)
                nc.vector.tensor_copy(h_plain[:, t, cols], acc[:])
            else:
                nc.scalar.activation(h_win[t][:, cols], acc[:], ACT.Copy, scale=-1.0)
                nc.scalar.copy(h_plain[:, t, cols], acc[:])

        h_product(0, halves[0])
        h_product(0, quarters[0])
        h_product(0, quarters[1], on_vector=True)
        for t in range(1, PACK):
            for cols in halves:
                h_product(t, cols)

        d6 = new("d6", [P, PACK, S], F32)
        d7 = new("d7", [P, PACK, S], F32)
        res = new("res", [P, PACK, S], F32)
        res_b = [new("res_b%d" % i, [P, HALF, PACK], BF16) for i in range(2)]
        res_c = new("res_c", [P, S], U32)
        res_s = new("res_s", [P, S], U8)
        out_rows = out_0.rearrange("(p t) n -> p t n", t=PACK)
        out_words = words(out_1)

        def step_diff(dst, lst, t, cols):
            nc.vector.tensor_tensor(dst[:, t, cols], h_win[t][:].indirect(entries(lst, cols)), h_plain[:, t, cols], ALU.add)

        def step_max(t, cols):
            nc.vector.tensor_tensor(res[:, t, cols], d6[:, t, cols], d7[:, t, cols], ALU.max)
            nc.sync.dma_start(out_rows[:, t, cols], res[:, t, cols])

        def planes_out(i):
            cols = halves[i]
            nc.vector.quantize_mx(
                res_c[:, cols].bitcast(FP8X4), res_s[:, cols], res_b[i][:].rearrange("p n t -> p (n t)")
            )
            nc.sync.dma_start(out_words[:, cols], res_c[:, cols].bitcast(I32))

        step_diff(d6, l6, 0, whole)
        step_diff(d7, l7, 0, whole)
        step_diff(d6, l6, 1, whole)
        step_max(0, whole)
        step_diff(d7, l7, 1, whole)
        step_diff(d6, l6, 2, whole)
        step_max(1, whole)
        for i, cols in enumerate(halves):
            weave(nc.scalar.copy, res_b[i], res, cols, low)
        step_diff(d7, l7, 2, whole)
        step_diff(d6, l6, 3, halves[0])
        step_max(2, whole)
        step_diff(d7, l7, 3, halves[0])
        step_diff(d6, l6, 3, halves[1])
        step_max(3, halves[0])
        weave(nc.scalar.copy, res_b[0], res, halves[0], high)
        step_diff(d7, l7, 3, halves[1])
        step_max(3, halves[1])
        planes_out(0)
        weave(nc.vector.tensor_copy, res_b[1], res, halves[1], high)
        planes_out(1)
        for q in range(4):
            queue = nc.sync if q < 2 else nc.scalar
            queue.dma_start(out_2[0, 4 * q : 4 * q + 4, :].bitcast(I32), res_s[32 * q : 32 * q + 4, :].bitcast(I32))
